import numpy as np, ml_dtypes
CORES = [23,119,17,113]
N = 4
QP = 256
def setup_inputs(rng):
    return {"q": rng.standard_normal((N, 128, QP), dtype=np.float32).astype(ml_dtypes.bfloat16), "k": rng.standard_normal((N, 128, 128), dtype=np.float32).astype(ml_dtypes.bfloat16), "v": rng.standard_normal((N, 128, 128), dtype=np.float32).astype(ml_dtypes.bfloat16)}
def setup_inputs_big(rng):
    d = setup_inputs(rng)
    for k in ("q", "k", "v"): d[k] = (d[k].astype(np.float32) * 1024.0).astype(d[k].dtype)
    return d
def setup_inputs_small(rng):
    d = setup_inputs(rng)
    for k in ("q", "k", "v"): d[k] = (d[k].astype(np.float32) * (1 / 1024.0)).astype(d[k].dtype)
    return d
def setup_inputs_apart(rng):
    d = setup_inputs(rng)
    f = (10.0 ** rng.permutation(np.linspace(-1.5, 1.5, N))).astype(np.float32).reshape(N, 1, 1)
    for k in ("q", "k", "v"): d[k] = (d[k].astype(np.float32) * f).astype(d[k].dtype)
    return d
def reference(q, k, v):
    Q, K, V = q.astype(np.float64), k.astype(np.float64), v.astype(np.float64)
    y = np.zeros((N, 128, QP))
    for r in range(N):
        S = [K[j].T @ Q[r] for j in range(N)]
        m = np.max([s.max(axis=0) for s in S], axis=0)
        y[r] = sum(V[j].T @ np.maximum(S[j] - 0.5 * m, 0.0) for j in range(N))
    return {"y": y.astype(ml_dtypes.bfloat16)}

@@ -1,0 +1,231 @@
+from concourse.bass import DstId, RemoteDMATransfer
+from concourse.mybir import AluOpType
+
+N = 4
+D = 128
+QP = 256
+W = 64
+
+SCRATCH = {
+    "q_sb": ("sbuf", [128, QP], "bfloat16"),
+    "kall": ("sbuf", [128, N * D], "bfloat16"),
+    "vall": ("sbuf", [128, N * D], "bfloat16"),
+    "ida": ("sbuf", [128, 136], "bfloat16"),
+    "idd": ("dram", [128 * 129], "bfloat16"),
+    "ident": ("sbuf", [128, 128], "bfloat16"),
+    "sel": ("sbuf", [128, 256], "bfloat16"),
+    "zeros": ("sbuf", [128, QP], "float32"),
+    "acc0": ("sbuf", [128, W], "float32"),
+    "acc1": ("sbuf", [128, W], "float32"),
+    "t32": ("sbuf", [128, 32], "float32"),
+    "t16": ("sbuf", [128, 16], "float32"),
+    "t8": ("sbuf", [128, 8], "float32"),
+    "t4": ("sbuf", [128, 4], "float32"),
+    "m2": ("sbuf", [128, 8], "bfloat16"),
+    "mrow": ("sbuf", [128, 128], "bfloat16"),
+    "p": ("sbuf", [128, N * QP], "bfloat16"),
+    "ysb": ("sbuf", [128, QP], "bfloat16"),
+    "s0": ("psum", [128, 512], "float32"),
+    "s1": ("psum", [128, 512], "float32"),
+    "s2": ("psum", [128, 512], "float32"),
+    "s3": ("psum", [128, 512], "float32"),
+    "x0": ("psum", [128, 512], "float32"),
+    "x1": ("psum", [128, 512], "float32"),
+    "x2": ("psum", [128, 512], "float32"),
+    "mt": ("psum", [128, 512], "float32"),
+}
+SEMAPHORES = (["kl", "ql", "vl", "idw", "idl", "ms", "sent", "dv", "mts", "mrs", "p3b", "y0", "y1", "c0", "c1",
+               "o0", "o1"]
+              + ["kr%d" % j for j in range(N)] + ["vr%d" % j for j in range(N)]
+              + ["st%d" % i for i in range(N)] + ["b%d" % i for i in range(N)] + ["p%d" % i for i in range(N)])
+
+
+def _bits(m):
+    return [e for e in range(m.bit_length()) if (m >> e) & 1]
+
+
+def _plan(topo, cores, r):
+    c = cores[r]
+    peers = [j for j in range(len(cores)) if j != r]
+    near = [j for j in peers if topo.chip(cores[j]) == topo.chip(c)]
+    far = [j for j in peers if topo.chip(cores[j]) != topo.chip(c)]
+    far.sort(key=lambda j: 0 if topo.die(cores[j]) == topo.die(c) else 1)
+    far_mask = 0
+    if far:
+        far_mask = topo.mask(c, cores[far[0]])
+        for j in far:
+            far_mask &= topo.mask(c, cores[j])
+    near_mask = 0
+    if near:
+        near_mask = topo.mask(c, cores[near[0]])
+        for j in near:
+            near_mask &= topo.mask(c, cores[j])
+        near_mask &= ~far_mask
+    return far, far_mask, near, near_mask
+
+
+def rank_program(g, core, T, topo):
+    rank = T.rank_of(core)
+    if rank is None:
+        return
+    cores = list(T.cores)
+    sem = T.sem
+    PE, V, SY, SC = g.tensor, g.vector, g.sync, g.scalar
+    MAX = AluOpType.max
+
+    far, far_mask, near, near_mask = _plan(topo, cores, rank)
+    order = [rank] + near + far
+
+    def arrives(s):
+        f, fm, n, nm = _plan(topo, cores, s)
+        return len(_bits(fm)) if rank in f else len(_bits(nm))
+
+    def blk(t, j, w=D):
+        return t[:, j * w:(j + 1) * w]
+
+    SY.dma_start(blk(T.kall, rank), T.k[:, :]).then_inc(sem.kl, 16)
+    SC.dma_start(blk(T.vall, rank), T.v[:, :]).then_inc(sem.vl, 16)
+    SY.dma_start(T.q_sb[:, :], T.q[:, :]).then_inc(sem.ql, 16)
+
+    def send(buf, name):
+        trs = []
+        for grp, mask in ((far, far_mask), (near, near_mask)):
+            if not grp:
+                continue
+            ids = []
+            for j in grp:
+                assert topo.may_write(core, cores[j])
+                rid, pid, _se = topo.addr(cores[j])
+                ids.append(DstId(rid=rid, pnc=pid))
+            trs.append(RemoteDMATransfer(dst_ids=ids, dma_engine_mask=mask, remote_sem=sem[name % rank],
+                                         srcs=[blk(buf, rank)], dsts=[blk(buf, rank) for _ in grp]))
+        g.remote_dma_fused(trs, local_sem=sem.sent)
+        return sum(len(_bits(m)) for grp, m in ((far, far_mask), (near, near_mask)) if grp)
+
+    g.wait_ge(sem.kl, 16)
+    left = send(T.kall, "kr%d")
+    g.wait_ge(sem.vl, 16)
+    left += send(T.vall, "vr%d")
+    g.wait_ge(sem.sent, left)
+
+    nms = [0]
+
+    def fill(ap, val):
+        if nms[0]:
+            V.wait_ge(sem.ms, nms[0])
+        V.memset(ap, val).then_inc(sem.ms, 1)
+        nms[0] += 1
+
+    fill(T.ida[:, :], 0.0)
+    fill(T.ida[:, 0:1], 1.0)
+    ms_id = nms[0]
+    fill(T.sel[0:2, 0:128], 0.0)
+    fill(T.sel[0:1, 0:128], -0.5)
+    fill(T.sel[0:2, 128:256], -0.5)
+    fill(T.sel[0:1, 128:256], 0.0)
+    fill(T.zeros[:, :], 0.0)
+    ms_all = nms[0]
+
+    SC.wait_ge(sem.ms, ms_id)
+    SC.dma_start(T.idd[0:128 * 129], T.ida[:, 0:129]).then_inc(sem.idw, 16)
+    SC.wait_ge(sem.idw, 16)
+    SC.dma_start(T.ident[:, :], T.idd[0:128 * 128]).then_inc(sem.idl, 16)
+
+    S = [T.s0, T.s1, T.s2, T.s3]
+    X = [T.x0, T.x1, T.x2, T.x0]
+    Y = [T.x1, T.x2]
+
+    def st_mm(i):
+        kj = blk(T.kall, order[i])
+        for h in range(2):
+            PE.matmul(blk(X[i], h), blk(T.q_sb, h), kj, True, True).then_inc(sem["st%d" % i], 1)
+
+    def s_mm(i):
+        PE.matmul(S[i][:, 0:QP], blk(T.kall, order[i]), T.q_sb[:, :], True, False)
+
+    PE.wait_ge(sem.kl, 16)
+    PE.wait_ge(sem.ql, 16)
+    st_mm(0)
+    s_mm(0)
+    PE.wait_ge(sem["kr%d" % order[1]], arrives(order[1]))
+    st_mm(1)
+    s_mm(1)
+    PE.wait_ge(sem["kr%d" % order[2]], arrives(order[2]))
+    st_mm(2)
+    PE.wait_ge(sem["kr%d" % order[3]], arrives(order[3]))
+    PE.wait_ge(sem.dv, 4)
+    st_mm(3)
+    s_mm(2)
+    s_mm(3)
+
+    ndv = [0]
+    acc = [T.acc0, T.acc1]
+
+    def chain(issue):
+        if ndv[0]:
+            V.wait_ge(sem.dv, ndv[0])
+        issue().then_inc(sem.dv, 1)
+        ndv[0] += 1
+
+    step = QP // W
+    for i in range(N):
+        V.wait_ge(sem["st%d" % i], 2)
+        for a in range(step):
+            src = X[i][:, a:QP:step]
+            n = ndv[0]
+            if n == 0:
+                chain(lambda: V.tensor_copy(acc[0][:, :], src))
+            else:
+                chain(lambda: V.tensor_tensor(acc[n % 2][:, :], src, acc[(n - 1) % 2][:, :], MAX))
+    cur, width = acc[(ndv[0] - 1) % 2], W
+    for nxt in (T.t32, T.t16, T.t8, T.t4, T.m2):
+        half = width // 2
+        c = cur
+        w = width
+        chain(lambda: V.tensor_tensor(nxt[:, 0:half], c[:, 0:w:2], c[:, 1:w:2], MAX))
+        cur, width = nxt, half
+    dv_all = ndv[0]
+
+    PE.wait_ge(sem.idl, 16)
+    PE.wait_ge(sem.ms, ms_all)
+    PE.wait_ge(sem.dv, dv_all)
+    PE.matmul(T.mt[0:2, 0:128], T.m2[:, 0:2], T.ident[:, :], True, True).then_inc(sem.mts, 1)
+    V.wait_ge(sem.mts, 1)
+    V.tensor_copy(T.mrow[0:2, :], T.mt[0:2, 0:128]).then_inc(sem.mrs, 1)
+    PE.wait_ge(sem.mrs, 1)
+    for i in range(N):
+        for h in range(2):
+            PE.matmul(blk(S[i], h), T.sel[0:2, h * 128:(h + 1) * 128], T.mrow[0:2, :],
+                      False, h == 1).then_inc(sem["b%d" % i], 1)
+
+    V.wait_ge(sem.ms, ms_all)
+    for i in range(N):
+        V.wait_ge(sem["b%d" % i], 2)
+        if i < N - 1:
+            V.tensor_tensor(blk(T.p, i, QP), S[i][:, 0:QP], T.zeros[:, :], MAX).then_inc(sem["p%d" % i], 1)
+        else:
+            for h, name in ((0, "p%d" % i), (1, "p3b")):
+                lo = i * QP + h * 128
+                V.tensor_tensor(T.p[:, lo:lo + 128], blk(S[i], h), blk(T.zeros, h), MAX).then_inc(sem[name], 1)
+
+    for i in range(N):
+        j = order[i]
+        if i == 0:
+            PE.wait_ge(sem.vl, 16)
+        else:
+            PE.wait_ge(sem["vr%d" % j], arrives(j))
+        PE.wait_ge(sem["p%d" % i], 1)
+        for h in range(2):
+            lo = i * QP + h * 128
+            if i == N - 1 and h == 1:
+                PE.wait_ge(sem.p3b, 1)
+            mm = PE.matmul(Y[h][:, 0:128], blk(T.vall, j), T.p[:, lo:lo + 128], i == 0, i == N - 1)
+            if i == N - 1:
+                mm.then_inc(sem["y%d" % h], 1)
+
+    for h, Q in ((0, SY), (1, SC)):
+        V.wait_ge(sem["y%d" % h], 1)
+        V.tensor_copy(blk(T.ysb, h), Y[h][:, 0:128]).then_inc(sem["c%d" % h], 1)
+        Q.wait_ge(sem["c%d" % h], 1)
+        Q.dma_start(blk(T.y, h), blk(T.ysb, h)).then_inc(sem["o%d" % h], 16)
+        Q.wait_ge(sem["o%d" % h], 16)

@@ -1,28 +1,21 @@
 from concourse.bass import DstId, RemoteDMATransfer
-from concourse.mybir import AluOpType
+from concourse.mybir import AluOpType, AxisListType, ActivationFunctionType
 
 N = 4
 D = 128
 QP = 256
-W = 64
+FAR_ENGINES = 8
+NEAR_ENGINES = 8
 
 SCRATCH = {
     "q_sb": ("sbuf", [128, QP], "bfloat16"),
-    "kall": ("sbuf", [128, N * D], "bfloat16"),
-    "vall": ("sbuf", [128, N * D], "bfloat16"),
-    "ida": ("sbuf", [128, 136], "bfloat16"),
-    "idd": ("dram", [128 * 129], "bfloat16"),
-    "ident": ("sbuf", [128, 128], "bfloat16"),
-    "sel": ("sbuf", [128, 256], "bfloat16"),
-    "zeros": ("sbuf", [128, QP], "float32"),
-    "acc0": ("sbuf", [128, W], "float32"),
-    "acc1": ("sbuf", [128, W], "float32"),
-    "t32": ("sbuf", [128, 32], "float32"),
-    "t16": ("sbuf", [128, 16], "float32"),
-    "t8": ("sbuf", [128, 8], "float32"),
-    "t4": ("sbuf", [128, 4], "float32"),
-    "m2": ("sbuf", [128, 8], "bfloat16"),
-    "mrow": ("sbuf", [128, 128], "bfloat16"),
+    "kv": ("sbuf", [128, N * 2 * D], "bfloat16"),
+    "nh": ("sbuf", [128, D], "bfloat16"),
+    "nid": ("sbuf", [128, D], "bfloat16"),
+    "ones": ("sbuf", [128, D], "bfloat16"),
+    "m0": ("sbuf", [128, 4], "float32"),
+    "m1": ("sbuf", [128, 4], "float32"),
+    "dg": ("sbuf", [128, QP], "bfloat16"),
     "p": ("sbuf", [128, N * QP], "bfloat16"),
     "ysb": ("sbuf", [128, QP], "bfloat16"),
     "s0": ("psum", [128, 512], "float32"),
@@ -31,17 +24,24 @@ SCRATCH = {
     "s3": ("psum", [128, 512], "float32"),
     "x0": ("psum", [128, 512], "float32"),
     "x1": ("psum", [128, 512], "float32"),
-    "x2": ("psum", [128, 512], "float32"),
-    "mt": ("psum", [128, 512], "float32"),
+    "xa": ("psum", [128, 512], "float32"),
+    "xb": ("psum", [128, 512], "float32"),
 }
-SEMAPHORES = (["kl", "ql", "vl", "idw", "idl", "ms", "sent", "dv", "mts", "mrs", "p3b", "y0", "y1", "c0", "c1",
-               "o0", "o1"]
+SEMAPHORES = (["kl", "ql", "vl", "ms", "idn", "sent", "dv", "sa", "sb", "r0", "r1", "d0", "d1", "y0", "y1",
+               "c0", "c1", "o0", "o1"]
               + ["kr%d" % j for j in range(N)] + ["vr%d" % j for j in range(N)]
-              + ["st%d" % i for i in range(N)] + ["b%d" % i for i in range(N)] + ["p%d" % i for i in range(N)])
+              + ["st%d" % i for i in range(N - 1)] + ["b%d" % i for i in range(N)] + ["p%d" % i for i in range(N)])
 
 
 def _bits(m):
     return [e for e in range(m.bit_length()) if (m >> e) & 1]
+
+
+def _take(m, n):
+    out = 0
+    for e in _bits(m)[:n]:
+        out |= 1 << e
+    return out
 
 
 def _plan(topo, cores, r):
@@ -50,18 +50,18 @@ def _plan(topo, cores, r):
     near = [j for j in peers if topo.chip(cores[j]) == topo.chip(c)]
     far = [j for j in peers if topo.chip(cores[j]) != topo.chip(c)]
     far.sort(key=lambda j: 0 if topo.die(cores[j]) == topo.die(c) else 1)
-    far_mask = 0
+    far_all = 0
     if far:
-        far_mask = topo.mask(c, cores[far[0]])
+        far_all = topo.mask(c, cores[far[0]])
         for j in far:
-            far_mask &= topo.mask(c, cores[j])
+            far_all &= topo.mask(c, cores[j])
     near_mask = 0
     if near:
         near_mask = topo.mask(c, cores[near[0]])
         for j in near:
             near_mask &= topo.mask(c, cores[j])
-        near_mask &= ~far_mask
-    return far, far_mask, near, near_mask
+        near_mask &= ~far_all
+    return far, _take(far_all, FAR_ENGINES), near, _take(near_mask, NEAR_ENGINES)
 
 
 def rank_program(g, core, T, topo):
@@ -71,161 +71,129 @@ def rank_program(g, core, T, topo):
     cores = list(T.cores)
     sem = T.sem
     PE, V, SY, SC = g.tensor, g.vector, g.sync, g.scalar
-    MAX = AluOpType.max
+    MAX, MULT = AluOpType.max, AluOpType.mult
+    AX = AxisListType.X
+    ACT = ActivationFunctionType
 
     far, far_mask, near, near_mask = _plan(topo, cores, rank)
     order = [rank] + near + far
+    n_far, n_near = len(_bits(far_mask)), len(_bits(near_mask))
 
-    def arrives(s):
-        f, fm, n, nm = _plan(topo, cores, s)
-        return len(_bits(fm)) if rank in f else len(_bits(nm))
+    def kb(j):
+        return T.kv[:, j * 2 * D:j * 2 * D + D]
+
+    def vb(j):
+        return T.kv[:, j * 2 * D + D:(j + 1) * 2 * D]
+
+    def kvb(j):
+        return T.kv[:, j * 2 * D:(j + 1) * 2 * D]
 
     def blk(t, j, w=D):
         return t[:, j * w:(j + 1) * w]
 
-    SY.dma_start(blk(T.kall, rank), T.k[:, :]).then_inc(sem.kl, 16)
-    SC.dma_start(blk(T.vall, rank), T.v[:, :]).then_inc(sem.vl, 16)
+    SY.dma_start(kb(rank), T.k[:, :]).then_inc(sem.kl, 16)
+    SC.dma_start(vb(rank), T.v[:, :]).then_inc(sem.vl, 16)
     SY.dma_start(T.q_sb[:, :], T.q[:, :]).then_inc(sem.ql, 16)
 
-    def send(buf, name):
-        trs = []
-        for grp, mask in ((far, far_mask), (near, near_mask)):
-            if not grp:
-                continue
-            ids = []
-            for j in grp:
-                assert topo.may_write(core, cores[j])
-                rid, pid, _se = topo.addr(cores[j])
-                ids.append(DstId(rid=rid, pnc=pid))
-            trs.append(RemoteDMATransfer(dst_ids=ids, dma_engine_mask=mask, remote_sem=sem[name % rank],
-                                         srcs=[blk(buf, rank)], dsts=[blk(buf, rank) for _ in grp]))
-        g.remote_dma_fused(trs, local_sem=sem.sent)
-        return sum(len(_bits(m)) for grp, m in ((far, far_mask), (near, near_mask)) if grp)
+    def send(ap, grp, mask, name):
+        ids = []
+        for j in grp:
+            assert topo.may_write(core, cores[j])
+            rid, pid, _se = topo.addr(cores[j])
+            ids.append(DstId(rid=rid, pnc=pid))
+        g.remote_dma_fused([RemoteDMATransfer(dst_ids=ids, dma_engine_mask=mask, remote_sem=sem[name % rank],
+                                              srcs=[ap], dsts=[ap for _ in grp])], local_sem=sem.sent)
+        return len(_bits(mask))
 
     g.wait_ge(sem.kl, 16)
-    left = send(T.kall, "kr%d")
+    left = send(kb(rank), far, far_mask, "kr%d")
     g.wait_ge(sem.vl, 16)
-    left += send(T.vall, "vr%d")
+    left += send(kvb(rank), near, near_mask, "kr%d")
+    left += send(vb(rank), far, far_mask, "vr%d")
+    g.wait_ge(sem.ms, 1)
+    g.affine_select(T.nid[:, :], T.nh[:, :], [[-1, D]], AluOpType.is_equal, 0.0, 0, 1).then_inc(sem.idn, 1)
     g.wait_ge(sem.sent, left)
 
-    nms = [0]
-
-    def fill(ap, val):
-        if nms[0]:
-            V.wait_ge(sem.ms, nms[0])
-        V.memset(ap, val).then_inc(sem.ms, 1)
-        nms[0] += 1
-
-    fill(T.ida[:, :], 0.0)
-    fill(T.ida[:, 0:1], 1.0)
-    ms_id = nms[0]
-    fill(T.sel[0:2, 0:128], 0.0)
-    fill(T.sel[0:1, 0:128], -0.5)
-    fill(T.sel[0:2, 128:256], -0.5)
-    fill(T.sel[0:1, 128:256], 0.0)
-    fill(T.zeros[:, :], 0.0)
-    ms_all = nms[0]
-
-    SC.wait_ge(sem.ms, ms_id)
-    SC.dma_start(T.idd[0:128 * 129], T.ida[:, 0:129]).then_inc(sem.idw, 16)
-    SC.wait_ge(sem.idw, 16)
-    SC.dma_start(T.ident[:, :], T.idd[0:128 * 128]).then_inc(sem.idl, 16)
-
     S = [T.s0, T.s1, T.s2, T.s3]
-    X = [T.x0, T.x1, T.x2, T.x0]
-    Y = [T.x1, T.x2]
+    X = [T.x0, T.x1, T.x0]
+    L = [T.xa, T.xb]
+    Y = [T.x0, T.x1]
 
     def st_mm(i):
-        kj = blk(T.kall, order[i])
         for h in range(2):
-            PE.matmul(blk(X[i], h), blk(T.q_sb, h), kj, True, True).then_inc(sem["st%d" % i], 1)
+            PE.matmul(blk(X[i], h), blk(T.q_sb, h), kb(order[i]), True, True).then_inc(sem["st%d" % i], 1)
 
     def s_mm(i):
-        PE.matmul(S[i][:, 0:QP], blk(T.kall, order[i]), T.q_sb[:, :], True, False)
+        PE.matmul(S[i][:, 0:QP], kb(order[i]), T.q_sb[:, :], True, False)
 
     PE.wait_ge(sem.kl, 16)
     PE.wait_ge(sem.ql, 16)
     st_mm(0)
     s_mm(0)
-    PE.wait_ge(sem["kr%d" % order[1]], arrives(order[1]))
+    PE.wait_ge(sem["kr%d" % order[1]], n_near)
     st_mm(1)
     s_mm(1)
-    PE.wait_ge(sem["kr%d" % order[2]], arrives(order[2]))
+    PE.wait_ge(sem["kr%d" % order[2]], n_far)
+    PE.wait_ge(sem.dv, 2)
     st_mm(2)
-    PE.wait_ge(sem["kr%d" % order[3]], arrives(order[3]))
-    PE.wait_ge(sem.dv, 4)
-    st_mm(3)
     s_mm(2)
+    PE.wait_ge(sem["kr%d" % order[3]], n_far)
+    PE.wait_ge(sem.dv, 6)
+    PE.matmul(L[0][:, 0:D], blk(T.q_sb, 0), kb(order[3]), True, True).then_inc(sem.sa, 1)
+    PE.matmul(L[1][:, 0:D], blk(T.q_sb, 1), kb(order[3]), True, True).then_inc(sem.sb, 1)
     s_mm(3)
 
-    ndv = [0]
-    acc = [T.acc0, T.acc1]
-
-    def chain(issue):
-        if ndv[0]:
-            V.wait_ge(sem.dv, ndv[0])
-        issue().then_inc(sem.dv, 1)
-        ndv[0] += 1
-
-    step = QP // W
-    for i in range(N):
+    V.memset(T.nh[:, :], -0.5).then_inc(sem.ms, 1)
+    V.memset(T.ones[:, :], 1.0).then_inc(sem.ms, 1)
+    for i in range(N - 1):
         V.wait_ge(sem["st%d" % i], 2)
-        for a in range(step):
-            src = X[i][:, a:QP:step]
-            n = ndv[0]
-            if n == 0:
-                chain(lambda: V.tensor_copy(acc[0][:, :], src))
-            else:
-                chain(lambda: V.tensor_tensor(acc[n % 2][:, :], src, acc[(n - 1) % 2][:, :], MAX))
-    cur, width = acc[(ndv[0] - 1) % 2], W
-    for nxt in (T.t32, T.t16, T.t8, T.t4, T.m2):
-        half = width // 2
-        c = cur
-        w = width
-        chain(lambda: V.tensor_tensor(nxt[:, 0:half], c[:, 0:w:2], c[:, 1:w:2], MAX))
-        cur, width = nxt, half
-    dv_all = ndv[0]
-
-    PE.wait_ge(sem.idl, 16)
-    PE.wait_ge(sem.ms, ms_all)
-    PE.wait_ge(sem.dv, dv_all)
-    PE.matmul(T.mt[0:2, 0:128], T.m2[:, 0:2], T.ident[:, :], True, True).then_inc(sem.mts, 1)
-    V.wait_ge(sem.mts, 1)
-    V.tensor_copy(T.mrow[0:2, :], T.mt[0:2, 0:128]).then_inc(sem.mrs, 1)
-    PE.wait_ge(sem.mrs, 1)
-    for i in range(N):
         for h in range(2):
-            PE.matmul(blk(S[i], h), T.sel[0:2, h * 128:(h + 1) * 128], T.mrow[0:2, :],
-                      False, h == 1).then_inc(sem["b%d" % i], 1)
+            V.tensor_reduce(L[h][:, D + i:D + i + 1], blk(X[i], h), AX, MAX).then_inc(sem.dv, 1)
+    V.wait_ge(sem.dv, 6)
+    V.wait_ge(sem.idn, 1)
+    M = [T.m0, T.m1]
+    for h, arrived, red, dia in ((0, sem.sa, sem.r0, sem.d0), (1, sem.sb, sem.r1, sem.d1)):
+        V.wait_ge(arrived, 1)
+        V.tensor_reduce(M[h][:, 0:1], L[h][:, 0:D + N - 1], AX, MAX).then_inc(red, 1)
+        V.wait_ge(red, 1)
+        V.tensor_scalar(blk(T.dg, h), T.nid[:, :], M[h][:, 0:1], None, MULT).then_inc(dia, 1)
 
-    V.wait_ge(sem.ms, ms_all)
+    PE.wait_ge(sem.ms, 2)
+    PE.wait_ge(sem.d0, 1)
     for i in range(N):
-        V.wait_ge(sem["b%d" % i], 2)
-        if i < N - 1:
-            V.tensor_tensor(blk(T.p, i, QP), S[i][:, 0:QP], T.zeros[:, :], MAX).then_inc(sem["p%d" % i], 1)
+        PE.matmul(blk(S[i], 0), T.ones[:, :], blk(T.dg, 0), False, False)
+    PE.wait_ge(sem.d1, 1)
+    for i in range(N):
+        PE.matmul(blk(S[i], 1), T.ones[:, :], blk(T.dg, 1), False, True).then_inc(sem["b%d" % i], 1)
+
+    for i in range(N):
+        if i % 2 == 0:
+            V.wait_ge(sem["b%d" % i], 1)
+            V.tensor_scalar(blk(T.p, i, QP), S[i][:, 0:QP], 0.0, None, MAX).then_inc(sem["p%d" % i], 1)
         else:
-            for h, name in ((0, "p%d" % i), (1, "p3b")):
-                lo = i * QP + h * 128
-                V.tensor_tensor(T.p[:, lo:lo + 128], blk(S[i], h), blk(T.zeros, h), MAX).then_inc(sem[name], 1)
+            SC.wait_ge(sem["b%d" % i], 1)
+            SC.activation(blk(T.p, i, QP), S[i][:, 0:QP], ACT.Relu).then_inc(sem["p%d" % i], 1)
 
     for i in range(N):
         j = order[i]
         if i == 0:
             PE.wait_ge(sem.vl, 16)
-        else:
-            PE.wait_ge(sem["vr%d" % j], arrives(j))
+        elif j in far:
+            PE.wait_ge(sem["vr%d" % j], n_far)
         PE.wait_ge(sem["p%d" % i], 1)
         for h in range(2):
-            lo = i * QP + h * 128
-            if i == N - 1 and h == 1:
-                PE.wait_ge(sem.p3b, 1)
-            mm = PE.matmul(Y[h][:, 0:128], blk(T.vall, j), T.p[:, lo:lo + 128], i == 0, i == N - 1)
+            lo = i * QP + h * D
+            mm = PE.matmul(Y[h][:, 0:D], vb(j), T.p[:, lo:lo + D], i == 0, i == N - 1)
             if i == N - 1:
                 mm.then_inc(sem["y%d" % h], 1)
 
-    for h, Q in ((0, SY), (1, SC)):
-        V.wait_ge(sem["y%d" % h], 1)
-        V.tensor_copy(blk(T.ysb, h), Y[h][:, 0:128]).then_inc(sem["c%d" % h], 1)
-        Q.wait_ge(sem["c%d" % h], 1)
-        Q.dma_start(blk(T.y, h), blk(T.ysb, h)).then_inc(sem["o%d" % h], 16)
-        Q.wait_ge(sem["o%d" % h], 16)
+    V.wait_ge(sem.y0, 1)
+    V.tensor_copy(blk(T.ysb, 0), Y[0][:, 0:D]).then_inc(sem.c0, 1)
+    SY.wait_ge(sem.c0, 1)
+    SY.dma_start(blk(T.y, 0), blk(T.ysb, 0)).then_inc(sem.o0, 16)
+    SY.wait_ge(sem.o0, 16)
+    SC.wait_ge(sem.y1, 1)
+    SC.activation(blk(T.ysb, 1), Y[1][:, 0:D], ACT.Copy).then_inc(sem.c1, 1)
+    SC.wait_ge(sem.c1, 1)
+    SC.dma_start(blk(T.y, 1), blk(T.ysb, 1)).then_inc(sem.o1, 16)
+    SC.wait_ge(sem.o1, 16)

@@ -4,10 +4,9 @@ from concourse.mybir import AluOpType, AxisListType, ActivationFunctionType
 N = 4
 D = 128
 QP = 256
-FAR_ENGINES = 8
-NEAR_ENGINES = 8
 
 SCRATCH = {
+    "kd": ("dram", [128, D], "bfloat16"),
     "q_sb": ("sbuf", [128, QP], "bfloat16"),
     "kv": ("sbuf", [128, N * 2 * D], "bfloat16"),
     "nh": ("sbuf", [128, D], "bfloat16"),
@@ -16,32 +15,32 @@ SCRATCH = {
     "m0": ("sbuf", [128, 4], "float32"),
     "m1": ("sbuf", [128, 4], "float32"),
     "dg": ("sbuf", [128, QP], "bfloat16"),
+    "ssb": ("sbuf", [128, (N - 1) * QP], "bfloat16"),
     "p": ("sbuf", [128, N * QP], "bfloat16"),
+    "r3": ("sbuf", [128, QP], "bfloat16"),
+    "wsb": ("sbuf", [128, 4], "float32"),
+    "wbb": ("sbuf", [128, QP], "float32"),
     "ysb": ("sbuf", [128, QP], "bfloat16"),
     "s0": ("psum", [128, 512], "float32"),
     "s1": ("psum", [128, 512], "float32"),
     "s2": ("psum", [128, 512], "float32"),
-    "s3": ("psum", [128, 512], "float32"),
     "x0": ("psum", [128, 512], "float32"),
     "x1": ("psum", [128, 512], "float32"),
     "xa": ("psum", [128, 512], "float32"),
     "xb": ("psum", [128, 512], "float32"),
+    "wb": ("psum", [128, 512], "float32"),
 }
-SEMAPHORES = (["kl", "ql", "vl", "ms", "idn", "sent", "dv", "sa", "sb", "r0", "r1", "d0", "d1", "y0", "y1",
-               "c0", "c1", "o0", "o1"]
+SEMAPHORES = (["kdl", "kl", "ql", "vl", "ms", "idn", "sent", "dv", "ws", "wc"]
               + ["kr%d" % j for j in range(N)] + ["vr%d" % j for j in range(N)]
-              + ["st%d" % i for i in range(N - 1)] + ["b%d" % i for i in range(N)] + ["p%d" % i for i in range(N)])
+              + ["st%d" % i for i in range(N - 1)] + ["ss%d" % i for i in range(N - 1)]
+              + ["cp%d" % i for i in range(N - 1)]
+              + ["%s%d" % (n, h) for n in ("a", "r", "d", "bb", "rl", "t", "c3", "wq", "y", "c", "o")
+                 for h in range(2)]
+              + ["pm%d%d" % (i, h) for i in range(N - 1) for h in range(2)])
 
 
 def _bits(m):
     return [e for e in range(m.bit_length()) if (m >> e) & 1]
-
-
-def _take(m, n):
-    out = 0
-    for e in _bits(m)[:n]:
-        out |= 1 << e
-    return out
 
 
 def _plan(topo, cores, r):
@@ -50,18 +49,13 @@ def _plan(topo, cores, r):
     near = [j for j in peers if topo.chip(cores[j]) == topo.chip(c)]
     far = [j for j in peers if topo.chip(cores[j]) != topo.chip(c)]
     far.sort(key=lambda j: 0 if topo.die(cores[j]) == topo.die(c) else 1)
-    far_all = 0
-    if far:
-        far_all = topo.mask(c, cores[far[0]])
-        for j in far:
-            far_all &= topo.mask(c, cores[j])
-    near_mask = 0
-    if near:
-        near_mask = topo.mask(c, cores[near[0]])
-        for j in near:
-            near_mask &= topo.mask(c, cores[j])
-        near_mask &= ~far_all
-    return far, _take(far_all, FAR_ENGINES), near, _take(near_mask, NEAR_ENGINES)
+    far_mask = topo.mask(c, cores[far[0]])
+    for j in far:
+        far_mask &= topo.mask(c, cores[j])
+    near_mask = topo.mask(c, cores[near[0]])
+    for j in near:
+        near_mask &= topo.mask(c, cores[j])
+    return far, far_mask, near, near_mask & ~far_mask
 
 
 def rank_program(g, core, T, topo):
@@ -71,7 +65,7 @@ def rank_program(g, core, T, topo):
     cores = list(T.cores)
     sem = T.sem
     PE, V, SY, SC = g.tensor, g.vector, g.sync, g.scalar
-    MAX, MULT = AluOpType.max, AluOpType.mult
+    MAX, MULT, SUB = AluOpType.max, AluOpType.mult, AluOpType.subtract
     AX = AxisListType.X
     ACT = ActivationFunctionType
 
@@ -91,57 +85,80 @@ def rank_program(g, core, T, topo):
     def blk(t, j, w=D):
         return t[:, j * w:(j + 1) * w]
 
+    SY.dma_start(T.kd[:, :], T.k[:, :]).then_inc(sem.kdl, 16)
     SY.dma_start(kb(rank), T.k[:, :]).then_inc(sem.kl, 16)
-    SC.dma_start(vb(rank), T.v[:, :]).then_inc(sem.vl, 16)
+    SY.dma_start(vb(rank), T.v[:, :]).then_inc(sem.vl, 16)
     SY.dma_start(T.q_sb[:, :], T.q[:, :]).then_inc(sem.ql, 16)
 
-    def send(ap, grp, mask, name):
+    def send(src, dst, grp, mask, name):
         ids = []
         for j in grp:
             assert topo.may_write(core, cores[j])
             rid, pid, _se = topo.addr(cores[j])
             ids.append(DstId(rid=rid, pnc=pid))
         g.remote_dma_fused([RemoteDMATransfer(dst_ids=ids, dma_engine_mask=mask, remote_sem=sem[name % rank],
-                                              srcs=[ap], dsts=[ap for _ in grp])], local_sem=sem.sent)
-        return len(_bits(mask))
+                                              srcs=[src], dsts=[dst for _ in grp])], local_sem=sem.sent)
 
+    g.wait_ge(sem.kdl, 16)
+    send(T.kd[:, :], kb(rank), far, far_mask, "kr%d")
     g.wait_ge(sem.kl, 16)
-    left = send(kb(rank), far, far_mask, "kr%d")
     g.wait_ge(sem.vl, 16)
-    left += send(kvb(rank), near, near_mask, "kr%d")
-    left += send(vb(rank), far, far_mask, "vr%d")
+    send(kvb(rank), kvb(rank), near, near_mask, "kr%d")
+    send(vb(rank), vb(rank), far, far_mask, "vr%d")
     g.wait_ge(sem.ms, 1)
     g.affine_select(T.nid[:, :], T.nh[:, :], [[-1, D]], AluOpType.is_equal, 0.0, 0, 1).then_inc(sem.idn, 1)
-    g.wait_ge(sem.sent, left)
+    g.wait_ge(sem.sent, 2 * n_far + n_near)
 
-    S = [T.s0, T.s1, T.s2, T.s3]
+    S = [T.s0, T.s1, T.s2]
     X = [T.x0, T.x1, T.x0]
     L = [T.xa, T.xb]
+    B = [T.s0, T.s1]
+    M = [T.m0, T.m1]
     Y = [T.x0, T.x1]
 
-    def st_mm(i):
+    def early(i):
         for h in range(2):
             PE.matmul(blk(X[i], h), blk(T.q_sb, h), kb(order[i]), True, True).then_inc(sem["st%d" % i], 1)
+        PE.matmul(S[i][:, 0:QP], kb(order[i]), T.q_sb[:, :], True, True).then_inc(sem["ss%d" % i], 1)
 
-    def s_mm(i):
-        PE.matmul(S[i][:, 0:QP], kb(order[i]), T.q_sb[:, :], True, False)
+    def w_mm(i):
+        return PE.matmul(T.wb[:, 0:1], vb(order[i]), T.ones[:, 0:1], i == 0, i == N - 2)
 
     PE.wait_ge(sem.kl, 16)
     PE.wait_ge(sem.ql, 16)
-    st_mm(0)
-    s_mm(0)
+    early(0)
+    PE.wait_ge(sem.vl, 16)
+    PE.wait_ge(sem.ms, 2)
+    w_mm(0)
     PE.wait_ge(sem["kr%d" % order[1]], n_near)
-    st_mm(1)
-    s_mm(1)
+    early(1)
+    w_mm(1)
     PE.wait_ge(sem["kr%d" % order[2]], n_far)
     PE.wait_ge(sem.dv, 2)
-    st_mm(2)
-    s_mm(2)
+    early(2)
     PE.wait_ge(sem["kr%d" % order[3]], n_far)
     PE.wait_ge(sem.dv, 6)
-    PE.matmul(L[0][:, 0:D], blk(T.q_sb, 0), kb(order[3]), True, True).then_inc(sem.sa, 1)
-    PE.matmul(L[1][:, 0:D], blk(T.q_sb, 1), kb(order[3]), True, True).then_inc(sem.sb, 1)
-    s_mm(3)
+    for h in range(2):
+        PE.matmul(L[h][:, 0:D], blk(T.q_sb, h), kb(order[3]), True, True).then_inc(sem["a%d" % h], 1)
+    PE.wait_ge(sem.idn, 1)
+    for h in range(2):
+        PE.wait_ge(sem["d%d" % h], 1)
+        PE.wait_ge(sem["cp%d" % h], 1)
+        PE.matmul(B[h][:, 0:D], T.ones[:, :], blk(T.dg, h), True, True).then_inc(sem["bb%d" % h], 1)
+        PE.wait_ge(sem["rl%d" % h], 1)
+        PE.matmul(L[h][:, 0:D], blk(T.r3, h), T.nid[:, :], True, True).then_inc(sem["t%d" % h], 1)
+    for h in range(2):
+        for i in range(N):
+            j = order[i]
+            if h == 0 and j in far:
+                PE.wait_ge(sem["vr%d" % j], n_far)
+            if h == 0 and i == N - 2:
+                w_mm(i).then_inc(sem.ws, 1)
+            PE.wait_ge(sem["pm%d%d" % (i, h)] if i < N - 1 else sem["c3%d" % h], 1)
+            lo = i * QP + h * D
+            mm = PE.matmul(Y[h][:, 0:D], vb(j), T.p[:, lo:lo + D], i == 0, i == N - 1)
+            if i == N - 1:
+                mm.then_inc(sem["y%d" % h], 1)
 
     V.memset(T.nh[:, :], -0.5).then_inc(sem.ms, 1)
     V.memset(T.ones[:, :], 1.0).then_inc(sem.ms, 1)
@@ -151,49 +168,44 @@ def rank_program(g, core, T, topo):
             V.tensor_reduce(L[h][:, D + i:D + i + 1], blk(X[i], h), AX, MAX).then_inc(sem.dv, 1)
     V.wait_ge(sem.dv, 6)
     V.wait_ge(sem.idn, 1)
-    M = [T.m0, T.m1]
-    for h, arrived, red, dia in ((0, sem.sa, sem.r0, sem.d0), (1, sem.sb, sem.r1, sem.d1)):
-        V.wait_ge(arrived, 1)
-        V.tensor_reduce(M[h][:, 0:1], L[h][:, 0:D + N - 1], AX, MAX).then_inc(red, 1)
-        V.wait_ge(red, 1)
-        V.tensor_scalar(blk(T.dg, h), T.nid[:, :], M[h][:, 0:1], None, MULT).then_inc(dia, 1)
-
-    PE.wait_ge(sem.ms, 2)
-    PE.wait_ge(sem.d0, 1)
-    for i in range(N):
-        PE.matmul(blk(S[i], 0), T.ones[:, :], blk(T.dg, 0), False, False)
-    PE.wait_ge(sem.d1, 1)
-    for i in range(N):
-        PE.matmul(blk(S[i], 1), T.ones[:, :], blk(T.dg, 1), False, True).then_inc(sem["b%d" % i], 1)
-
-    for i in range(N):
-        if i % 2 == 0:
-            V.wait_ge(sem["b%d" % i], 1)
-            V.tensor_scalar(blk(T.p, i, QP), S[i][:, 0:QP], 0.0, None, MAX).then_inc(sem["p%d" % i], 1)
-        else:
-            SC.wait_ge(sem["b%d" % i], 1)
-            SC.activation(blk(T.p, i, QP), S[i][:, 0:QP], ACT.Relu).then_inc(sem["p%d" % i], 1)
-
-    for i in range(N):
-        j = order[i]
-        if i == 0:
-            PE.wait_ge(sem.vl, 16)
-        elif j in far:
-            PE.wait_ge(sem["vr%d" % j], n_far)
-        PE.wait_ge(sem["p%d" % i], 1)
-        for h in range(2):
+    for h in range(2):
+        V.wait_ge(sem["a%d" % h], 1)
+        V.tensor_reduce(M[h][:, 0:1], L[h][:, 0:D + N - 1], AX, MAX, negate=True).then_inc(sem["r%d" % h], 1)
+        V.wait_ge(sem["r%d" % h], 1)
+        V.tensor_scalar(blk(T.dg, h), T.nid[:, :], M[h][:, 0:1], None, MULT).then_inc(sem["d%d" % h], 1)
+    for h in range(2):
+        V.wait_ge(sem["bb%d" % h], 1)
+        for i in range(N - 1):
+            if h == 0:
+                V.wait_ge(sem["cp%d" % i], 1)
             lo = i * QP + h * D
-            mm = PE.matmul(Y[h][:, 0:D], vb(j), T.p[:, lo:lo + D], i == 0, i == N - 1)
-            if i == N - 1:
-                mm.then_inc(sem["y%d" % h], 1)
+            V.tensor_tensor(T.p[:, lo:lo + D], T.ssb[:, lo:lo + D], B[h][:, 0:D], MAX).then_inc(
+                sem["pm%d%d" % (i, h)], 1)
+    for h in range(2):
+        V.wait_ge(sem["wq%d" % h], 1)
+        V.wait_ge(sem["y%d" % h], 1)
+        V.tensor_tensor(blk(T.ysb, h), Y[h][:, 0:D], blk(T.wbb, h), SUB).then_inc(sem["c%d" % h], 1)
 
-    V.wait_ge(sem.y0, 1)
-    V.tensor_copy(blk(T.ysb, 0), Y[0][:, 0:D]).then_inc(sem.c0, 1)
-    SY.wait_ge(sem.c0, 1)
-    SY.dma_start(blk(T.y, 0), blk(T.ysb, 0)).then_inc(sem.o0, 16)
-    SY.wait_ge(sem.o0, 16)
-    SC.wait_ge(sem.y1, 1)
-    SC.activation(blk(T.ysb, 1), Y[1][:, 0:D], ACT.Copy).then_inc(sem.c1, 1)
-    SC.wait_ge(sem.c1, 1)
-    SC.dma_start(blk(T.y, 1), blk(T.ysb, 1)).then_inc(sem.o1, 16)
-    SC.wait_ge(sem.o1, 16)
+    for i in range(N - 1):
+        SC.wait_ge(sem["ss%d" % i], 1)
+        SC.activation(blk(T.ssb, i, QP), S[i][:, 0:QP], ACT.Copy).then_inc(sem["cp%d" % i], 1)
+    for h in range(2):
+        SC.wait_ge(sem["r%d" % h], 1)
+        SC.activation(blk(T.r3, h), L[h][:, 0:D], ACT.Relu, bias=M[h][:, 0:1], scale=2.0).then_inc(
+            sem["rl%d" % h], 1)
+    for h in range(2):
+        SC.wait_ge(sem["t%d" % h], 1)
+        lo = (N - 1) * QP + h * D
+        SC.activation(T.p[:, lo:lo + D], L[h][:, 0:D], ACT.Copy, scale=-1.0).then_inc(sem["c3%d" % h], 1)
+    SC.wait_ge(sem.ws, 1)
+    SC.activation(T.wsb[:, 0:1], T.wb[:, 0:1], ACT.Copy).then_inc(sem.wc, 1)
+    SC.wait_ge(sem.wc, 1)
+    for h in range(2):
+        for i in range(N - 1):
+            SC.wait_ge(sem["pm%d%d" % (i, h)], 1)
+        SC.activation(blk(T.wbb, h), B[h][:, 0:D], ACT.Identity, scale=T.wsb[:, 0:1]).then_inc(sem["wq%d" % h], 1)
+
+    for h, Q in ((0, SY), (1, SC)):
+        Q.wait_ge(sem["c%d" % h], 1)
+        Q.dma_start(blk(T.y, h), blk(T.ysb, h)).then_inc(sem["o%d" % h], 16)
+        Q.wait_ge(sem["o%d" % h], 16)

from concourse.bass import DstId, RemoteDMATransfer
from concourse.mybir import AluOpType, AxisListType, ActivationFunctionType

N = 4
D = 128
QP = 256

SCRATCH = {
    "kd": ("dram", [128, D], "bfloat16"),
    "q_sb": ("sbuf", [128, QP], "bfloat16"),
    "kv": ("sbuf", [128, N * 2 * D], "bfloat16"),
    "nh": ("sbuf", [128, D], "bfloat16"),
    "nid": ("sbuf", [128, D], "bfloat16"),
    "ones": ("sbuf", [128, D], "bfloat16"),
    "m0": ("sbuf", [128, 4], "float32"),
    "m1": ("sbuf", [128, 4], "float32"),
    "dg": ("sbuf", [128, QP], "bfloat16"),
    "ssb": ("sbuf", [128, (N - 1) * QP], "bfloat16"),
    "p": ("sbuf", [128, N * QP], "bfloat16"),
    "r3": ("sbuf", [128, QP], "bfloat16"),
    "wsb": ("sbuf", [128, 4], "float32"),
    "wbb": ("sbuf", [128, QP], "float32"),
    "ysb": ("sbuf", [128, QP], "bfloat16"),
    "s0": ("psum", [128, 512], "float32"),
    "s1": ("psum", [128, 512], "float32"),
    "s2": ("psum", [128, 512], "float32"),
    "x0": ("psum", [128, 512], "float32"),
    "x1": ("psum", [128, 512], "float32"),
    "xa": ("psum", [128, 512], "float32"),
    "xb": ("psum", [128, 512], "float32"),
    "wb": ("psum", [128, 512], "float32"),
}
SEMAPHORES = (["kdl", "kl", "ql", "vl", "ms", "idn", "sent", "dv", "ws", "wc"]
              + ["kr%d" % j for j in range(N)] + ["vr%d" % j for j in range(N)]
              + ["st%d" % i for i in range(N - 1)] + ["ss%d" % i for i in range(N - 1)]
              + ["cp%d" % i for i in range(N - 1)]
              + ["%s%d" % (n, h) for n in ("a", "r", "d", "bb", "rl", "t", "c3", "wq", "y", "c", "o")
                 for h in range(2)]
              + ["pm%d%d" % (i, h) for i in range(N - 1) for h in range(2)])


def _bits(m):
    return [e for e in range(m.bit_length()) if (m >> e) & 1]


def _plan(topo, cores, r):
    c = cores[r]
    peers = [j for j in range(len(cores)) if j != r]
    near = [j for j in peers if topo.chip(cores[j]) == topo.chip(c)]
    far = [j for j in peers if topo.chip(cores[j]) != topo.chip(c)]
    far.sort(key=lambda j: 0 if topo.die(cores[j]) == topo.die(c) else 1)
    far_mask = topo.mask(c, cores[far[0]])
    for j in far:
        far_mask &= topo.mask(c, cores[j])
    near_mask = topo.mask(c, cores[near[0]])
    for j in near:
        near_mask &= topo.mask(c, cores[j])
    return far, far_mask, near, near_mask & ~far_mask


def rank_program(g, core, T, topo):
    rank = T.rank_of(core)
    if rank is None:
        return
    cores = list(T.cores)
    sem = T.sem
    PE, V, SY, SC = g.tensor, g.vector, g.sync, g.scalar
    MAX, MULT, SUB = AluOpType.max, AluOpType.mult, AluOpType.subtract
    AX = AxisListType.X
    ACT = ActivationFunctionType

    far, far_mask, near, near_mask = _plan(topo, cores, rank)
    order = [rank] + near + far
    n_far, n_near = len(_bits(far_mask)), len(_bits(near_mask))

    def kb(j):
        return T.kv[:, j * 2 * D:j * 2 * D + D]

    def vb(j):
        return T.kv[:, j * 2 * D + D:(j + 1) * 2 * D]

    def kvb(j):
        return T.kv[:, j * 2 * D:(j + 1) * 2 * D]

    def blk(t, j, w=D):
        return t[:, j * w:(j + 1) * w]

    SY.dma_start(T.kd[:, :], T.k[:, :]).then_inc(sem.kdl, 16)
    SY.dma_start(kb(rank), T.k[:, :]).then_inc(sem.kl, 16)
    SY.dma_start(vb(rank), T.v[:, :]).then_inc(sem.vl, 16)
    SY.dma_start(T.q_sb[:, :], T.q[:, :]).then_inc(sem.ql, 16)

    def send(src, dst, grp, mask, name):
        ids = []
        for j in grp:
            assert topo.may_write(core, cores[j])
            rid, pid, _se = topo.addr(cores[j])
            ids.append(DstId(rid=rid, pnc=pid))
        g.remote_dma_fused([RemoteDMATransfer(dst_ids=ids, dma_engine_mask=mask, remote_sem=sem[name % rank],
                                              srcs=[src], dsts=[dst for _ in grp])], local_sem=sem.sent)

    g.wait_ge(sem.kdl, 16)
    send(T.kd[:, :], kb(rank), far, far_mask, "kr%d")
    g.wait_ge(sem.kl, 16)
    g.wait_ge(sem.vl, 16)
    send(kvb(rank), kvb(rank), near, near_mask, "kr%d")
    send(vb(rank), vb(rank), far, far_mask, "vr%d")
    g.wait_ge(sem.ms, 1)
    g.affine_select(T.nid[:, :], T.nh[:, :], [[-1, D]], AluOpType.is_equal, 0.0, 0, 1).then_inc(sem.idn, 1)
    g.wait_ge(sem.sent, 2 * n_far + n_near)

    S = [T.s0, T.s1, T.s2]
    X = [T.x0, T.x1, T.x0]
    L = [T.xa, T.xb]
    B = [T.s0, T.s1]
    M = [T.m0, T.m1]
    Y = [T.x0, T.x1]

    def early(i):
        for h in range(2):
            PE.matmul(blk(X[i], h), blk(T.q_sb, h), kb(order[i]), True, True).then_inc(sem["st%d" % i], 1)
        PE.matmul(S[i][:, 0:QP], kb(order[i]), T.q_sb[:, :], True, True).then_inc(sem["ss%d" % i], 1)

    def w_mm(i):
        return PE.matmul(T.wb[:, 0:1], vb(order[i]), T.ones[:, 0:1], i == 0, i == N - 2)

    PE.wait_ge(sem.kl, 16)
    PE.wait_ge(sem.ql, 16)
    early(0)
    PE.wait_ge(sem.vl, 16)
    PE.wait_ge(sem.ms, 2)
    w_mm(0)
    PE.wait_ge(sem["kr%d" % order[1]], n_near)
    early(1)
    w_mm(1)
    PE.wait_ge(sem["kr%d" % order[2]], n_far)
    PE.wait_ge(sem.dv, 2)
    early(2)
    PE.wait_ge(sem["kr%d" % order[3]], n_far)
    PE.wait_ge(sem.dv, 6)
    for h in range(2):
        PE.matmul(L[h][:, 0:D], blk(T.q_sb, h), kb(order[3]), True, True).then_inc(sem["a%d" % h], 1)
    PE.wait_ge(sem.idn, 1)
    for h in range(2):
        PE.wait_ge(sem["d%d" % h], 1)
        PE.wait_ge(sem["cp%d" % h], 1)
        PE.matmul(B[h][:, 0:D], T.ones[:, :], blk(T.dg, h), True, True).then_inc(sem["bb%d" % h], 1)
        PE.wait_ge(sem["rl%d" % h], 1)
        PE.matmul(L[h][:, 0:D], blk(T.r3, h), T.nid[:, :], True, True).then_inc(sem["t%d" % h], 1)
    for h in range(2):
        for i in range(N):
            j = order[i]
            if h == 0 and j in far:
                PE.wait_ge(sem["vr%d" % j], n_far)
            if h == 0 and i == N - 2:
                w_mm(i).then_inc(sem.ws, 1)
            PE.wait_ge(sem["pm%d%d" % (i, h)] if i < N - 1 else sem["c3%d" % h], 1)
            lo = i * QP + h * D
            mm = PE.matmul(Y[h][:, 0:D], vb(j), T.p[:, lo:lo + D], i == 0, i == N - 1)
            if i == N - 1:
                mm.then_inc(sem["y%d" % h], 1)

    V.memset(T.nh[:, :], -0.5).then_inc(sem.ms, 1)
    V.memset(T.ones[:, :], 1.0).then_inc(sem.ms, 1)
    for i in range(N - 1):
        V.wait_ge(sem["st%d" % i], 2)
        for h in range(2):
            V.tensor_reduce(L[h][:, D + i:D + i + 1], blk(X[i], h), AX, MAX).then_inc(sem.dv, 1)
    V.wait_ge(sem.dv, 6)
    V.wait_ge(sem.idn, 1)
    for h in range(2):
        V.wait_ge(sem["a%d" % h], 1)
        V.tensor_reduce(M[h][:, 0:1], L[h][:, 0:D + N - 1], AX, MAX, negate=True).then_inc(sem["r%d" % h], 1)
        V.wait_ge(sem["r%d" % h], 1)
        V.tensor_scalar(blk(T.dg, h), T.nid[:, :], M[h][:, 0:1], None, MULT).then_inc(sem["d%d" % h], 1)
    for h in range(2):
        V.wait_ge(sem["bb%d" % h], 1)
        for i in range(N - 1):
            if h == 0:
                V.wait_ge(sem["cp%d" % i], 1)
            lo = i * QP + h * D
            V.tensor_tensor(T.p[:, lo:lo + D], T.ssb[:, lo:lo + D], B[h][:, 0:D], MAX).then_inc(
                sem["pm%d%d" % (i, h)], 1)
    for h in range(2):
        V.wait_ge(sem["wq%d" % h], 1)
        V.wait_ge(sem["y%d" % h], 1)
        V.tensor_tensor(blk(T.ysb, h), Y[h][:, 0:D], blk(T.wbb, h), SUB).then_inc(sem["c%d" % h], 1)

    for i in range(N - 1):
        SC.wait_ge(sem["ss%d" % i], 1)
        SC.activation(blk(T.ssb, i, QP), S[i][:, 0:QP], ACT.Copy).then_inc(sem["cp%d" % i], 1)
    for h in range(2):
        SC.wait_ge(sem["r%d" % h], 1)
        SC.activation(blk(T.r3, h), L[h][:, 0:D], ACT.Relu, bias=M[h][:, 0:1], scale=2.0).then_inc(
            sem["rl%d" % h], 1)
    for h in range(2):
        SC.wait_ge(sem["t%d" % h], 1)
        lo = (N - 1) * QP + h * D
        SC.activation(T.p[:, lo:lo + D], L[h][:, 0:D], ACT.Copy, scale=-1.0).then_inc(sem["c3%d" % h], 1)
    SC.wait_ge(sem.ws, 1)
    SC.activation(T.wsb[:, 0:1], T.wb[:, 0:1], ACT.Copy).then_inc(sem.wc, 1)
    SC.wait_ge(sem.wc, 1)
    for h in range(2):
        for i in range(N - 1):
            SC.wait_ge(sem["pm%d%d" % (i, h)], 1)
        SC.activation(blk(T.wbb, h), B[h][:, 0:D], ACT.Identity, scale=T.wsb[:, 0:1]).then_inc(sem["wq%d" % h], 1)

    for h, Q in ((0, SY), (1, SC)):
        Q.wait_ge(sem["c%d" % h], 1)
        Q.dma_start(blk(T.y, h), blk(T.ysb, h)).then_inc(sem["o%d" % h], 16)
        Q.wait_ge(sem["o%d" % h], 16)
